import numpy as np
import ml_dtypes


def mxq(x, axis, fmt="e4m3"):
    dtype, down = {"e4m3": (ml_dtypes.float8_e4m3fn, 7), "e5m2": (ml_dtypes.float8_e5m2, 14)}[fmt]
    v = np.moveaxis(np.asarray(x, np.float32).astype(ml_dtypes.bfloat16).astype(np.float64), axis, -1)
    blocks = v.reshape(v.shape[:-1] + (-1, 32))
    amax = np.abs(blocks).max(-1, keepdims=True)
    byte = np.maximum(np.where(amax > 0, np.frexp(amax)[1] - 1 + 127, 0) - down, 1)
    scale = np.exp2(byte - 127.0)
    codes = (blocks / scale).astype(np.float32).astype(dtype).astype(np.float64)
    return np.moveaxis((codes * scale).reshape(v.shape), -1, axis)


WIDE = False


def mx_kscale(k):
    if not WIDE:
        return np.ones(k)
    levels = np.array([10, -10, 5, -5, 0])
    if k % 512:
        return np.exp2(np.random.permutation(np.resize(levels, k // 32))).repeat(32)
    a = np.empty((k // 512, 16))
    for p in range(k // 512):
        a[p, :8] = np.random.permutation(np.resize(levels, 8))
        for g in range(8):
            far = levels[np.abs(levels - a[p, g]) >= 10]
            a[p, g + 8] = far[np.random.randint(len(far))]
    return np.exp2(a.ravel()).repeat(32)


def f64(x):
    return np.asarray(x).astype(np.float64)


def striped(idx):
    return np.tile(idx.reshape(-1, 16).T, (8, 1)).astype(np.uint16)


def unstriped(offs):
    return offs[:16].T.reshape(-1).astype(np.int64)


def striped8(idx):
    return np.concatenate([x.reshape(-1, 16).T for x in idx]).astype(np.uint16)


def runs(offs, k):
    lists = np.stack([offs[16 * r : 16 * r + 16].T.reshape(-1) for r in range(8)]).astype(np.int64)
    return lists[np.arange(k) % 512 // 64]


def pack_weight(w):
    k, n = w.shape
    w = f64(np.asarray(w, np.float32).astype(ml_dtypes.bfloat16)).reshape(k // 32, 32, n)
    amax = np.abs(w).max(1)
    byte = np.clip(np.where(amax > 0, np.frexp(amax)[1] - 1 + 127 - 7, 1), 1, 254)
    scaled = (w * np.exp2(127.0 - byte)[:, None, :]).reshape(k, n).astype(np.float32)
    words = np.ascontiguousarray(scaled.reshape(k // 512, 128, 4, n).transpose(0, 1, 3, 2)).astype(ml_dtypes.float8_e4m3fn).view(np.uint8)
    return words, np.ascontiguousarray(byte.astype(np.uint8).reshape(k // 512, 16, n))


def unpack_weight(words, scales):
    g, p, n, _ = words.shape
    vals = np.ascontiguousarray(words).view(ml_dtypes.float8_e4m3fn).astype(np.float64) * np.repeat(np.exp2(scales.astype(np.float64) - 127.0), 8, axis=1)[..., None]
    return vals.transpose(0, 1, 3, 2).reshape(g * 512, n)


K, T, S, H, W, C = 512, 2048, 512, 512, 256, 512


def setup_inputs():
    n = np.random.standard_normal
    s = mx_kscale(K)[:, None]
    packed_xT = pack_weight(n((K, T)) * s)
    return {
        "x_words": packed_xT[0],
        "x_scales": packed_xT[1],
        "w1": (n((K, H)) / np.sqrt(K) / s).astype(np.float32),
        "w2": (n((K, H)) / np.sqrt(K) / s).astype(np.float32),
        "gs": (np.random.uniform(0.5, 1.5, (K, 1)) / s).astype(np.float32),
        "offs": striped(np.random.permutation(T)[:S]),
        "two": striped(np.random.permutation(T)[:S]),
        "n1": striped8(np.stack([np.random.permutation(S)[:W] for _ in range(8)])),
        "n2": striped8(np.stack([np.random.permutation(S)[:W] for _ in range(8)])),
        "cand": striped(np.random.permutation(T)[:C]),
        "n3": striped8(np.stack([np.random.permutation(S) for _ in range(8)])),
        "n4": striped8(np.stack([np.random.permutation(S) for _ in range(8)])),
        "n5": striped8(np.stack([np.random.permutation(S) for _ in range(8)])),
    }


def reference(x_words, x_scales, w1, w2, gs, offs, two, n1, n2, cand, n3, n4, n5):
    x_cand = unpack_weight(x_words, x_scales)[:, unstriped(cand)]
    x_two = unpack_weight(x_words, x_scales)[:, unstriped(two)]
    d = mxq(f64(w2), 0, "e4m3").T @ x_two
    xq = unpack_weight(x_words, x_scales)[:, unstriped(offs)]
    y = mxq(f64(w1), 0, "e4m3").T @ xq
    ra = d[np.arange(H)[:, None], runs(n2, H)] - (0.5 * (y[np.arange(H)[:, None], runs(n1, H)]))
    ds = y.copy()
    ds[np.arange(H)[:, None], runs(n1, H)] = ra
    z = f64(gs) * ds
    s = 0.0625 * ((x_cand.T @ mxq(z, 0, "e4m3")))
    ex = np.exp(0.5 * s)
    return np.log((ex + ex[np.arange(C)[:, None], runs(n3, C)]) / (ex[np.arange(C)[:, None], runs(n4, C)] + ex[np.arange(C)[:, None], runs(n5, C)]))

@@ -1,0 +1,176 @@
+from contextlib import ExitStack
+
+import concourse.mybir as mybir
+
+K, T, S, H, W, C = 512, 2048, 512, 512, 256, 512
+P = 128
+PACK = 4
+FLOPS = 3 * 2 * K * H * S
+
+F32 = mybir.dt.float32
+BF16 = mybir.dt.bfloat16
+I32 = mybir.dt.int32
+U32 = mybir.dt.uint32
+U16 = mybir.dt.uint16
+U8 = mybir.dt.uint8
+FP8X4 = mybir.dt.float8_e4m3fn_x4
+ACT = mybir.ActivationFunctionType
+ALU = mybir.AluOpType
+SCALAR_TILES = (2, 3)
+
+
+def tile_picked_twcputbodds_none_p_kernel(tc, x_words, x_scales, w1, w2, gs, offs, two, n1, n2, cand, n3, n4, n5, out):
+    nc = tc.nc
+    with ExitStack() as ctx:
+        keep = ctx.enter_context(tc.tile_pool(name="keep", bufs=1))
+        psum = ctx.enter_context(tc.psum_pool(name="psum", bufs=1))
+
+        def load_list(src, name):
+            tile = keep.tile(list(src.shape), U16, name=name)
+            nc.sync.dma_start(tile[:], src)
+            return tile
+
+        def load_weight_half(w, half, name):
+            raw = keep.tile([P, PACK, H // 2], F32, name=name, tag=name, align_bytes=64)
+            cols = slice(half * H // 2, (half + 1) * H // 2)
+            nc.sync.dma_start(raw[:], w.rearrange("(p j) c -> p j c", j=PACK)[:, :, cols])
+            return raw
+
+        words = keep.tile([P, T], I32, name="words", align_bytes=64)
+        scales = keep.tile([P, T], U8, name="scales", align_bytes=64)
+        nc.vector.memset(scales[:].bitcast(I32), 0)
+        nc.sync.dma_start(words[:], x_words[0].rearrange("p n r -> p (n r)").bitcast(I32))
+        offs_t = load_list(offs, "offs_t")
+        for q in range(4):
+            nc.scalar.dma_start(scales[32 * q : 32 * q + 4, :].bitcast(I32), x_scales[0, 4 * q : 4 * q + 4, :].bitcast(I32))
+        w1_raw = [load_weight_half(w1, h, "w1_raw%d" % h) for h in range(2)]
+        two_t = load_list(two, "two_t")
+        w2_raw = [load_weight_half(w2, h, "w2_raw%d" % h) for h in range(2)]
+        n1_t = load_list(n1, "n1_t")
+        n2_t = load_list(n2, "n2_t")
+        gs_t = keep.tile([P, PACK], F32, name="gs_t")
+        nc.sync.dma_start(gs_t[:], gs.rearrange("(p t) o -> p (t o)", t=PACK))
+        cand_t = load_list(cand, "cand_t")
+        n3_t = load_list(n3, "n3_t")
+        n4_t = load_list(n4, "n4_t")
+        n5_t = load_list(n5, "n5_t")
+
+        ex = [keep.tile([P, 2 * S], F32, name="ex%d" % t) for t in range(PACK)]
+        half_s = {t: keep.tile([P, 2 * S], F32, name="half_s%d" % t, tag="half_s%d" % t) for t in SCALAR_TILES}
+        for t in range(PACK):
+            nc.gpsimd.memset(ex[t][:, S:], 0.0)
+        for t in SCALAR_TILES:
+            nc.gpsimd.memset(half_s[t][:, S:], 0.0)
+
+        def gather_words(lst, name):
+            got = keep.tile([P, S], U32, name=name, align_bytes=64)
+            nc.vector.tensor_copy(got[:], words[:].bitcast(U32).indirect(lst[:]))
+            return got
+
+        def gather_scales(lst, name, tag):
+            got = keep.tile([P, S], U8, name=name, tag=tag, align_bytes=64)
+            nc.vector.tensor_copy(got[:], scales[:].indirect(lst[:]))
+            return got
+
+        def round_weight(raw, name):
+            grouped = keep.tile([P, PACK, P, PACK], BF16, name=name, align_bytes=64)
+            for h in range(2):
+                nc.scalar.copy(
+                    grouped[:, :, h * P // 2 : (h + 1) * P // 2, :].rearrange("p t m j -> p m j t"),
+                    raw[h][:].rearrange("p j (m t) -> p m j t", t=PACK),
+                )
+            return grouped
+
+        def quantize(flat, name):
+            codes = keep.tile([P, S], U32, name=name + "_codes", align_bytes=64)
+            plane = keep.tile([P, S], U8, name=name + "_plane", align_bytes=64)
+            nc.vector.quantize_mx(out=codes[:].bitcast(FP8X4), scales=plane[:], in_=flat)
+            return codes, plane
+
+        def product(bank, t, lhs, rhs):
+            cols = slice(t * P, (t + 1) * P)
+            nc.tensor.matmul_mx(bank[:], lhsT=lhs[0][:, cols].bitcast(FP8X4), lhsT_scale=lhs[1][:, cols],
+                                rhs=rhs[0][:].bitcast(FP8X4), rhs_scale=rhs[1][:], start=True, stop=True)
+
+        xq = (gather_words(offs_t, "xq_w"), gather_scales(offs_t, "xq_s", "xq_s"))
+        w1_g = round_weight(w1_raw, "w1_g")
+        xt = (gather_words(two_t, "xt_w"), gather_scales(two_t, "xt_s", "xt_s"))
+        w1_q = quantize(w1_g[:].rearrange("p t m j -> p (t m j)"), "w1")
+        w2_g = round_weight(w2_raw, "w2_g")
+
+        y = [keep.tile([P, S], F32, name="y%d" % t) for t in range(PACK)]
+        d = [keep.tile([P, S], F32, name="d%d" % t, tag="d%d" % t, align_bytes=64) for t in range(PACK)]
+        a = [keep.tile([P, W], F32, name="a%d" % t) for t in range(PACK)]
+        b = [keep.tile([P, W], F32, name="b%d" % t) for t in range(PACK)]
+        for t in range(PACK):
+            bank = psum.tile([P, S], F32, name="bank_y%d" % t, tag="bank%d" % t)
+            product(bank, t, w1_q, xq)
+            nc.scalar.copy(y[t][:], bank[:])
+        nc.vector.tensor_scalar(a[0][:], y[0][:].indirect(n1_t[:]), -0.5, 0.0, ALU.mult, ALU.add)
+        w2_q = quantize(w2_g[:].rearrange("p t m j -> p (t m j)"), "w2")
+        for t in range(1, PACK):
+            nc.vector.tensor_scalar(a[t][:], y[t][:].indirect(n1_t[:]), -0.5, 0.0, ALU.mult, ALU.add)
+        for t in range(PACK):
+            bank = psum.tile([P, S], F32, name="bank_d%d" % t, tag="bank%d" % (PACK + t))
+            product(bank, t, w2_q, xt)
+            nc.scalar.copy(d[t][:], bank[:])
+        z_g = keep.tile([P, S, PACK], BF16, name="z_g", align_bytes=64)
+        nc.vector.tensor_copy(b[0][:], d[0][:].indirect(n2_t[:]))
+        for t in range(PACK):
+            if t + 1 < PACK:
+                nc.vector.tensor_copy(b[t + 1][:], d[t + 1][:].indirect(n2_t[:]))
+            nc.vector.tensor_tensor(y[t][:].indirect(n1_t[:]), a[t][:], b[t][:], ALU.add)
+            parts = 2 if t == PACK - 1 else 1
+            for h in range(parts):
+                cols = slice(h * S // parts, (h + 1) * S // parts)
+                nc.scalar.activation(z_g[:, cols, t], y[t][:, cols], ACT.Copy, scale=gs_t[:, t : t + 1])
+
+        xc_w = keep.tile([P, C], U32, name="xc_w", tag="d3", align_bytes=64)
+        nc.vector.tensor_copy(xc_w[:].rearrange("p (t m) -> p m t", t=PACK), words[:].bitcast(U32).indirect(cand_t[:]))
+        xc_plain = gather_scales(cand_t, "xc_plain", "w1_raw1")
+        xc_s = keep.tile([P, C], U8, name="xc_s", align_bytes=64)
+        nc.vector.tensor_copy(xc_s[:].rearrange("p (t m) -> p m t", t=PACK), xc_plain[:].rearrange("p (m t) -> p m t", t=PACK))
+        z_codes = keep.tile([P, S], U32, name="z_codes", align_bytes=64)
+        z_plane = keep.tile([P, S], U8, name="z_plane", align_bytes=64)
+        for h in range(2):
+            cols = slice(h * S // 2, (h + 1) * S // 2)
+            nc.vector.quantize_mx(out=z_codes[:, cols].bitcast(FP8X4), scales=z_plane[:, cols], in_=z_g[:, cols, :].rearrange("p j t -> p (j t)"))
+        z_q = (z_codes, z_plane)
+
+        own = [keep.tile([P, S], F32, name="own%d" % t) for t in range(PACK)]
+        e4 = [keep.tile([P, S], F32, name="e4_%d" % t) for t in range(PACK)]
+        e3 = {t: keep.tile([P, S], F32, name="e3_%d" % t) for t in SCALAR_TILES}
+        sums = [keep.tile([P, 2, S], F32, name="sums%d" % t) for t in range(PACK)]
+        banks = {}
+        for t in (0, 2, 3, 1):
+            bank = psum.tile([P, S], F32, name="bank_s%d" % t, tag="bank%d" % t)
+            product(bank, t, (xc_w, xc_s), z_q)
+            banks[t] = bank
+        for t in SCALAR_TILES:
+            nc.vector.tensor_scalar(half_s[t][:, :S], banks[t][:], 0.03125, None, ALU.mult)
+        for t in range(PACK):
+            if t not in SCALAR_TILES:
+                nc.scalar.activation(own[t][:], banks[t][:], ACT.Exp, scale=0.03125)
+            nc.scalar.activation(ex[t][:, :S], banks[t][:], ACT.Exp, scale=0.03125)
+        for t in SCALAR_TILES:
+            nc.scalar.activation(e4[t][:], half_s[t][:].indirect(n4_t[:]), ACT.Exp)
+            nc.scalar.activation(e3[t][:], half_s[t][:].indirect(n3_t[:]), ACT.Exp)
+        for t in range(PACK):
+            if t in SCALAR_TILES:
+                nc.vector.tensor_tensor(sums[t][:, 1, :], ex[t][:].indirect(n5_t[:]), e4[t][:], ALU.add)
+                nc.vector.tensor_tensor(sums[t][:, 0, :], ex[t][:, :S], e3[t][:], ALU.add)
+            else:
+                nc.vector.tensor_copy(e4[t][:], ex[t][:].indirect(n4_t[:]))
+                nc.vector.tensor_tensor(sums[t][:, 0, :], ex[t][:].indirect(n3_t[:]), own[t][:], ALU.add)
+                nc.vector.tensor_tensor(sums[t][:, 1, :], ex[t][:].indirect(n5_t[:]), e4[t][:], ALU.add)
+        rows = out.rearrange("(p t) j -> p t j", t=PACK)
+        all_logs = keep.tile([P, PACK, 2, S], F32, name="all_logs", tag="half_s3")
+        for t in range(PACK):
+            logs = all_logs[:, t]
+            res = keep.tile([P, S], F32, name="res%d" % t)
+            parts = 2 if t == PACK - 1 else 1
+            for h in range(parts):
+                cols = slice(h * S // parts, (h + 1) * S // parts)
+                nc.scalar.activation(logs[:, :, cols], sums[t][:, :, cols], ACT.Ln)
+                nc.vector.tensor_tensor(res[:, cols], logs[:, 0, cols], logs[:, 1, cols], ALU.subtract)
+                nc.sync.dma_start(rows[:, t, cols], res[:, cols])

@@ -1,6 +1,7 @@
 from contextlib import ExitStack
 
 import concourse.mybir as mybir
+from concourse.masks import make_identity
 
 K, T, S, H, W, C = 512, 2048, 512, 512, 256, 512
 P = 128
@@ -38,32 +39,35 @@ def tile_picked_twcputbodds_none_p_kernel(tc, x_words, x_scales, w1, w2, gs, off
 
         words = keep.tile([P, T], I32, name="words", align_bytes=64)
         scales = keep.tile([P, T], U8, name="scales", align_bytes=64)
-        nc.vector.memset(scales[:].bitcast(I32), 0)
-        nc.sync.dma_start(words[:], x_words[0].rearrange("p n r -> p (n r)").bitcast(I32))
+        nc.gpsimd.memset(scales[:, : T // 4].bitcast(I32), 0)
+        nc.vector.memset(scales[:, T // 4 :].bitcast(I32), 0)
         offs_t = load_list(offs, "offs_t")
-        for q in range(4):
-            nc.scalar.dma_start(scales[32 * q : 32 * q + 4, :].bitcast(I32), x_scales[0, 4 * q : 4 * q + 4, :].bitcast(I32))
-        w1_raw = [load_weight_half(w1, h, "w1_raw%d" % h) for h in range(2)]
         two_t = load_list(two, "two_t")
+        cand_t = load_list(cand, "cand_t")
+        for q in range(4):
+            nc.sync.dma_start(scales[32 * q : 32 * q + 4, :].bitcast(I32), x_scales[0, 4 * q : 4 * q + 4, :].bitcast(I32))
+        w1_whole = keep.tile([P, PACK, H], F32, name="w1_whole")
+        nc.sync.dma_start(w1_whole[:], w1.rearrange("(p j) c -> p j c", j=PACK))
+        w1_raw = [w1_whole[:, :, h * H // 2 : (h + 1) * H // 2] for h in range(2)]
+        nc.sync.dma_start(words[:], x_words[0].rearrange("p n r -> p (n r)").bitcast(I32))
         w2_raw = [load_weight_half(w2, h, "w2_raw%d" % h) for h in range(2)]
         n1_t = load_list(n1, "n1_t")
         n2_t = load_list(n2, "n2_t")
         gs_t = keep.tile([P, PACK], F32, name="gs_t")
         nc.sync.dma_start(gs_t[:], gs.rearrange("(p t) o -> p (t o)", t=PACK))
-        cand_t = load_list(cand, "cand_t")
         n3_t = load_list(n3, "n3_t")
         n4_t = load_list(n4, "n4_t")
         n5_t = load_list(n5, "n5_t")
 
-        ex = [keep.tile([P, 2 * S], F32, name="ex%d" % t) for t in range(PACK)]
-        half_s = {t: keep.tile([P, 2 * S], F32, name="half_s%d" % t, tag="half_s%d" % t) for t in SCALAR_TILES}
-        for t in range(PACK):
-            nc.gpsimd.memset(ex[t][:, S:], 0.0)
-        for t in SCALAR_TILES:
-            nc.gpsimd.memset(half_s[t][:, S:], 0.0)
+        ex = [keep.tile([P, S if t == PACK - 1 else 2 * S], F32, name="ex%d" % t) for t in range(PACK)]
+        last_ab = keep.tile([P, S], F32, name="last_ab", tag="last_ab", align_bytes=64)
+        ab = [ex[t][:, S:] for t in range(PACK - 1)] + [last_ab[:]]
+        half_s = {t: w2_raw[i][:].rearrange("p j c -> p (j c)") for i, t in enumerate(SCALAR_TILES)}
+        ident = keep.tile([P, P], F32, name="ident")
+        make_identity(nc, ident[:])
 
-        def gather_words(lst, name):
-            got = keep.tile([P, S], U32, name=name, align_bytes=64)
+        def gather_words(lst, name, tag):
+            got = keep.tile([P, S], U32, name=name, tag=tag, align_bytes=64)
             nc.vector.tensor_copy(got[:], words[:].bitcast(U32).indirect(lst[:]))
             return got
 
@@ -72,12 +76,12 @@ def tile_picked_twcputbodds_none_p_kernel(tc, x_words, x_scales, w1, w2, gs, off
             nc.vector.tensor_copy(got[:], scales[:].indirect(lst[:]))
             return got
 
-        def round_weight(raw, name):
-            grouped = keep.tile([P, PACK, P, PACK], BF16, name=name, align_bytes=64)
+        def round_weight(raw, name, movers):
+            grouped = keep.tile([P, PACK, P, PACK], BF16, name=name, tag=name, align_bytes=64)
             for h in range(2):
-                nc.scalar.copy(
+                movers[h](
                     grouped[:, :, h * P // 2 : (h + 1) * P // 2, :].rearrange("p t m j -> p m j t"),
-                    raw[h][:].rearrange("p j (m t) -> p m j t", t=PACK),
+                    raw[h].rearrange("p j (m t) -> p m j t", t=PACK),
                 )
             return grouped
 
@@ -87,49 +91,51 @@ def tile_picked_twcputbodds_none_p_kernel(tc, x_words, x_scales, w1, w2, gs, off
             nc.vector.quantize_mx(out=codes[:].bitcast(FP8X4), scales=plane[:], in_=flat)
             return codes, plane
 
-        def product(bank, t, lhs, rhs):
+        def product(bank, t, lhs, rhs, places=slice(0, S)):
             cols = slice(t * P, (t + 1) * P)
-            nc.tensor.matmul_mx(bank[:], lhsT=lhs[0][:, cols].bitcast(FP8X4), lhsT_scale=lhs[1][:, cols],
-                                rhs=rhs[0][:].bitcast(FP8X4), rhs_scale=rhs[1][:], start=True, stop=True)
+            nc.tensor.matmul_mx(bank[:, places], lhsT=lhs[0][:, cols].bitcast(FP8X4), lhsT_scale=lhs[1][:, cols],
+                                rhs=rhs[0][:, places].bitcast(FP8X4), rhs_scale=rhs[1][:, places], start=True, stop=True)
 
-        xq = (gather_words(offs_t, "xq_w"), gather_scales(offs_t, "xq_s", "xq_s"))
-        w1_g = round_weight(w1_raw, "w1_g")
-        xt = (gather_words(two_t, "xt_w"), gather_scales(two_t, "xt_s", "xt_s"))
+        xq_s = gather_scales(offs_t, "xq_s", "xq_s")
+        xt_s = gather_scales(two_t, "xt_s", "xt_s")
+        xc_plain = gather_scales(cand_t, "xc_plain", "xc_plain")
+        xc_s = keep.tile([P, C], U8, name="xc_s", align_bytes=64)
+        nc.vector.tensor_copy(xc_s[:].rearrange("p (t m) -> p m t", t=PACK), xc_plain[:].rearrange("p (m t) -> p m t", t=PACK))
+        w1_g = round_weight(w1_raw, "w1_g", (nc.scalar.copy, nc.scalar.copy))
         w1_q = quantize(w1_g[:].rearrange("p t m j -> p (t m j)"), "w1")
-        w2_g = round_weight(w2_raw, "w2_g")
+        xq = (gather_words(offs_t, "xq_w", "xq_w"), xq_s)
+        xt = (gather_words(two_t, "xt_w", "w1_g"), xt_s)
+        w2_g = round_weight([r[:] for r in w2_raw], "w2_g", (nc.scalar.copy, nc.scalar.copy))
 
         y = [keep.tile([P, S], F32, name="y%d" % t) for t in range(PACK)]
         d = [keep.tile([P, S], F32, name="d%d" % t, tag="d%d" % t, align_bytes=64) for t in range(PACK)]
-        a = [keep.tile([P, W], F32, name="a%d" % t) for t in range(PACK)]
-        b = [keep.tile([P, W], F32, name="b%d" % t) for t in range(PACK)]
+        a = [ab[t][:, :W] for t in range(PACK)]
+        b = [ab[t][:, W:] for t in range(PACK)]
         for t in range(PACK):
             bank = psum.tile([P, S], F32, name="bank_y%d" % t, tag="bank%d" % t)
             product(bank, t, w1_q, xq)
             nc.scalar.copy(y[t][:], bank[:])
-        nc.vector.tensor_scalar(a[0][:], y[0][:].indirect(n1_t[:]), -0.5, 0.0, ALU.mult, ALU.add)
+        nc.vector.tensor_scalar(a[0], y[0][:].indirect(n1_t[:]), -0.5, 0.0, ALU.mult, ALU.add)
         w2_q = quantize(w2_g[:].rearrange("p t m j -> p (t m j)"), "w2")
         for t in range(1, PACK):
-            nc.vector.tensor_scalar(a[t][:], y[t][:].indirect(n1_t[:]), -0.5, 0.0, ALU.mult, ALU.add)
+            nc.vector.tensor_scalar(a[t], y[t][:].indirect(n1_t[:]), -0.5, 0.0, ALU.mult, ALU.add)
         for t in range(PACK):
             bank = psum.tile([P, S], F32, name="bank_d%d" % t, tag="bank%d" % (PACK + t))
             product(bank, t, w2_q, xt)
             nc.scalar.copy(d[t][:], bank[:])
         z_g = keep.tile([P, S, PACK], BF16, name="z_g", align_bytes=64)
-        nc.vector.tensor_copy(b[0][:], d[0][:].indirect(n2_t[:]))
+        nc.vector.tensor_copy(b[0], d[0][:].indirect(n2_t[:]))
         for t in range(PACK):
             if t + 1 < PACK:
-                nc.vector.tensor_copy(b[t + 1][:], d[t + 1][:].indirect(n2_t[:]))
-            nc.vector.tensor_tensor(y[t][:].indirect(n1_t[:]), a[t][:], b[t][:], ALU.add)
+                nc.vector.tensor_copy(b[t + 1], d[t + 1][:].indirect(n2_t[:]))
+            nc.vector.tensor_tensor(y[t][:].indirect(n1_t[:]), a[t], b[t], ALU.add)
             parts = 2 if t == PACK - 1 else 1
             for h in range(parts):
                 cols = slice(h * S // parts, (h + 1) * S // parts)
                 nc.scalar.activation(z_g[:, cols, t], y[t][:, cols], ACT.Copy, scale=gs_t[:, t : t + 1])
 
-        xc_w = keep.tile([P, C], U32, name="xc_w", tag="d3", align_bytes=64)
+        xc_w = keep.tile([P, C], U32, name="xc_w", tag="last_ab", align_bytes=64)
         nc.vector.tensor_copy(xc_w[:].rearrange("p (t m) -> p m t", t=PACK), words[:].bitcast(U32).indirect(cand_t[:]))
-        xc_plain = gather_scales(cand_t, "xc_plain", "w1_raw1")
-        xc_s = keep.tile([P, C], U8, name="xc_s", align_bytes=64)
-        nc.vector.tensor_copy(xc_s[:].rearrange("p (t m) -> p m t", t=PACK), xc_plain[:].rearrange("p (m t) -> p m t", t=PACK))
         z_codes = keep.tile([P, S], U32, name="z_codes", align_bytes=64)
         z_plane = keep.tile([P, S], U8, name="z_plane", align_bytes=64)
         for h in range(2):
@@ -137,40 +143,49 @@ def tile_picked_twcputbodds_none_p_kernel(tc, x_words, x_scales, w1, w2, gs, off
             nc.vector.quantize_mx(out=z_codes[:, cols].bitcast(FP8X4), scales=z_plane[:, cols], in_=z_g[:, cols, :].rearrange("p j t -> p (j t)"))
         z_q = (z_codes, z_plane)
 
-        own = [keep.tile([P, S], F32, name="own%d" % t) for t in range(PACK)]
         e4 = [keep.tile([P, S], F32, name="e4_%d" % t) for t in range(PACK)]
-        e3 = {t: keep.tile([P, S], F32, name="e3_%d" % t) for t in SCALAR_TILES}
-        sums = [keep.tile([P, 2, S], F32, name="sums%d" % t) for t in range(PACK)]
-        banks = {}
-        for t in (0, 2, 3, 1):
-            bank = psum.tile([P, S], F32, name="bank_s%d" % t, tag="bank%d" % t)
-            product(bank, t, (xc_w, xc_s), z_q)
-            banks[t] = bank
+        e3 = [keep.tile([P, S], F32, name="e3_%d" % t) for t in range(PACK)]
+        den = [keep.tile([P, S], F32, name="den%d" % t) for t in range(PACK)]
+        banks = [psum.tile([P, S], F32, name="bank_s%d" % t, tag="bank%d" % t) for t in range(PACK)]
+        for h in range(2):
+            for t in (2, 0, 3, 1):
+                product(banks[t], t, (xc_w, xc_s), z_q, slice(h * S // 2, (h + 1) * S // 2))
         for t in SCALAR_TILES:
             nc.vector.tensor_scalar(half_s[t][:, :S], banks[t][:], 0.03125, None, ALU.mult)
         for t in range(PACK):
-            if t not in SCALAR_TILES:
-                nc.scalar.activation(own[t][:], banks[t][:], ACT.Exp, scale=0.03125)
             nc.scalar.activation(ex[t][:, :S], banks[t][:], ACT.Exp, scale=0.03125)
         for t in SCALAR_TILES:
-            nc.scalar.activation(e4[t][:], half_s[t][:].indirect(n4_t[:]), ACT.Exp)
-            nc.scalar.activation(e3[t][:], half_s[t][:].indirect(n3_t[:]), ACT.Exp)
+            nc.scalar.activation(e4[t][:], half_s[t].indirect(n4_t[:]), ACT.Exp)
+            nc.scalar.activation(e3[t][:], half_s[t].indirect(n3_t[:]), ACT.Exp)
+        num_t = []
         for t in range(PACK):
-            if t in SCALAR_TILES:
-                nc.vector.tensor_tensor(sums[t][:, 1, :], ex[t][:].indirect(n5_t[:]), e4[t][:], ALU.add)
-                nc.vector.tensor_tensor(sums[t][:, 0, :], ex[t][:, :S], e3[t][:], ALU.add)
-            else:
+            if t not in SCALAR_TILES:
                 nc.vector.tensor_copy(e4[t][:], ex[t][:].indirect(n4_t[:]))
-                nc.vector.tensor_tensor(sums[t][:, 0, :], ex[t][:].indirect(n3_t[:]), own[t][:], ALU.add)
-                nc.vector.tensor_tensor(sums[t][:, 1, :], ex[t][:].indirect(n5_t[:]), e4[t][:], ALU.add)
+                nc.vector.tensor_copy(e3[t][:], ex[t][:].indirect(n3_t[:]))
+            parts = 2 if t == PACK - 1 else 1
+            for h in range(parts):
+                cols = slice(h * S // parts, (h + 1) * S // parts)
+                entries = slice(h * S // parts // 16, (h + 1) * S // parts // 16)
+                nc.vector.tensor_tensor(den[t][:, cols], ex[t][:].indirect(n5_t[:, entries]), e4[t][:, cols], ALU.add)
+            bank = psum.tile([P, S], F32, name="bank_n%d" % t, tag="bank%d" % (PACK + t))
+            for c in range(S // P):
+                cols = slice(c * P, (c + 1) * P)
+                nc.tensor.matmul(bank[:, cols], ex[t][:, cols], ident[:], start=True, stop=False, is_transpose=True)
+                nc.tensor.matmul(bank[:, cols], e3[t][:, cols], ident[:], start=False, stop=True, is_transpose=True)
+            num_t.append(bank)
         rows = out.rearrange("(p t) j -> p t j", t=PACK)
-        all_logs = keep.tile([P, PACK, 2, S], F32, name="all_logs", tag="half_s3")
+        all_logs = keep.tile([P, PACK, 2, S], F32, name="all_logs", tag="w2_raw1", align_bytes=64)
         for t in range(PACK):
             logs = all_logs[:, t]
+            nc.scalar.activation(logs[:, 0, :], num_t[t][:], ACT.Ln)
+            bank = psum.tile([P, S], F32, name="bank_l%d" % t, tag="bank%d" % t)
+            for c in range(S // P):
+                cols = slice(c * P, (c + 1) * P)
+                nc.tensor.transpose(bank[:, cols], logs[:, 0, cols], ident[:])
             res = keep.tile([P, S], F32, name="res%d" % t)
             parts = 2 if t == PACK - 1 else 1
             for h in range(parts):
                 cols = slice(h * S // parts, (h + 1) * S // parts)
-                nc.scalar.activation(logs[:, :, cols], sums[t][:, :, cols], ACT.Ln)
-                nc.vector.tensor_tensor(res[:, cols], logs[:, 0, cols], logs[:, 1, cols], ALU.subtract)
+                nc.scalar.activation(logs[:, 1, cols], den[t][:, cols], ACT.Ln)
+                nc.vector.tensor_tensor(res[:, cols], bank[:, cols], logs[:, 1, cols], ALU.subtract)
                 nc.sync.dma_start(rows[:, t, cols], res[:, cols])

@@ -100,21 +100,24 @@ def tile_picked_twcputbodds_none_p_kernel(tc, x_words, x_scales, w1, w2, gs, off
         xt_s = gather_scales(two_t, "xt_s", "xt_s")
         xc_plain = gather_scales(cand_t, "xc_plain", "xc_plain")
         xc_s = keep.tile([P, C], U8, name="xc_s", align_bytes=64)
-        nc.vector.tensor_copy(xc_s[:].rearrange("p (t m) -> p m t", t=PACK), xc_plain[:].rearrange("p (m t) -> p m t", t=PACK))
+        nc.vector.tensor_copy(xc_s[:].rearrange("p (t m) -> p t m", t=PACK), xc_plain[:].rearrange("p (m t) -> p t m", t=PACK))
         w1_g = round_weight(w1_raw, "w1_g", (nc.scalar.copy, nc.scalar.copy))
         w1_q = quantize(w1_g[:].rearrange("p t m j -> p (t m j)"), "w1")
         xq = (gather_words(offs_t, "xq_w", "xq_w"), xq_s)
         xt = (gather_words(two_t, "xt_w", "w1_g"), xt_s)
         w2_g = round_weight([r[:] for r in w2_raw], "w2_g", (nc.scalar.copy, nc.scalar.copy))
 
-        y = [keep.tile([P, S], F32, name="y%d" % t) for t in range(PACK)]
+        y = [keep.tile([P, S + 1 if t < 2 else S], F32, name="y%d" % t) for t in range(PACK)]
+        for t in range(2):
+            nc.gpsimd.tensor_copy(y[t][:, S:], gs_t[:, t + 2 : t + 3])
+        d_gain = [gs_t[:, 0:1], gs_t[:, 1:2], y[0][:, S:], y[1][:, S:]]
         d = [keep.tile([P, S], F32, name="d%d" % t, tag="d%d" % t, align_bytes=64) for t in range(PACK)]
         a = [ab[t][:, :W] for t in range(PACK)]
         b = [ab[t][:, W:] for t in range(PACK)]
         for t in range(PACK):
             bank = psum.tile([P, S], F32, name="bank_y%d" % t, tag="bank%d" % t)
             product(bank, t, w1_q, xq)
-            nc.scalar.copy(y[t][:], bank[:])
+            nc.scalar.activation(y[t][:, :S], bank[:], ACT.Copy, scale=gs_t[:, t : t + 1])
         nc.vector.tensor_scalar(a[0], y[0][:].indirect(n1_t[:]), -0.5, 0.0, ALU.mult, ALU.add)
         w2_q = quantize(w2_g[:].rearrange("p t m j -> p (t m j)"), "w2")
         for t in range(1, PACK):
@@ -122,7 +125,7 @@ def tile_picked_twcputbodds_none_p_kernel(tc, x_words, x_scales, w1, w2, gs, off
         for t in range(PACK):
             bank = psum.tile([P, S], F32, name="bank_d%d" % t, tag="bank%d" % (PACK + t))
             product(bank, t, w2_q, xt)
-            nc.scalar.copy(d[t][:], bank[:])
+            nc.scalar.activation(d[t][:], bank[:], ACT.Copy, scale=d_gain[t])
         z_g = keep.tile([P, S, PACK], BF16, name="z_g", align_bytes=64)
         nc.vector.tensor_copy(b[0], d[0][:].indirect(n2_t[:]))
         for t in range(PACK):
@@ -132,7 +135,7 @@ def tile_picked_twcputbodds_none_p_kernel(tc, x_words, x_scales, w1, w2, gs, off
             parts = 2 if t == PACK - 1 else 1
             for h in range(parts):
                 cols = slice(h * S // parts, (h + 1) * S // parts)
-                nc.scalar.activation(z_g[:, cols, t], y[t][:, cols], ACT.Copy, scale=gs_t[:, t : t + 1])
+                nc.scalar.copy(z_g[:, cols, t], y[t][:, cols])
 
         xc_w = keep.tile([P, C], U32, name="xc_w", tag="last_ab", align_bytes=64)
         nc.vector.tensor_copy(xc_w[:].rearrange("p (t m) -> p m t", t=PACK), words[:].bitcast(U32).indirect(cand_t[:]))
@@ -148,11 +151,13 @@ def tile_picked_twcputbodds_none_p_kernel(tc, x_words, x_scales, w1, w2, gs, off
         den = [keep.tile([P, S], F32, name="den%d" % t) for t in range(PACK)]
         banks = [psum.tile([P, S], F32, name="bank_s%d" % t, tag="bank%d" % t) for t in range(PACK)]
         for h in range(2):
-            for t in (2, 0, 3, 1):
+            for t in (2, 0):
                 product(banks[t], t, (xc_w, xc_s), z_q, slice(h * S // 2, (h + 1) * S // 2))
+        for t in (3, 1):
+            product(banks[t], t, (xc_w, xc_s), z_q)
         for t in SCALAR_TILES:
             nc.vector.tensor_scalar(half_s[t][:, :S], banks[t][:], 0.03125, None, ALU.mult)
-        for t in range(PACK):
+        for t in (0, 2, 1, 3):
             nc.scalar.activation(ex[t][:, :S], banks[t][:], ACT.Exp, scale=0.03125)
         for t in SCALAR_TILES:
             nc.scalar.activation(e4[t][:], half_s[t].indirect(n4_t[:]), ACT.Exp)

@@ -153,12 +153,12 @@ def tile_picked_twcputbodds_none_p_kernel(tc, x_words, x_scales, w1, w2, gs, off
         for h in range(2):
             for t in (2, 0):
                 product(banks[t], t, (xc_w, xc_s), z_q, slice(h * S // 2, (h + 1) * S // 2))
-        for t in (3, 1):
+        for t in (1, 3):
             product(banks[t], t, (xc_w, xc_s), z_q)
-        for t in SCALAR_TILES:
-            nc.vector.tensor_scalar(half_s[t][:, :S], banks[t][:], 0.03125, None, ALU.mult)
+        nc.vector.tensor_scalar(half_s[2][:, :S], banks[2][:], 0.03125, None, ALU.mult)
         for t in (0, 2, 1, 3):
             nc.scalar.activation(ex[t][:, :S], banks[t][:], ACT.Exp, scale=0.03125)
+        nc.scalar.activation(half_s[3][:, :S], banks[3][:], ACT.Copy, scale=0.03125)
         for t in SCALAR_TILES:
             nc.scalar.activation(e4[t][:], half_s[t].indirect(n4_t[:]), ACT.Exp)
             nc.scalar.activation(e3[t][:], half_s[t].indirect(n3_t[:]), ACT.Exp)
@@ -180,17 +180,24 @@ def tile_picked_twcputbodds_none_p_kernel(tc, x_words, x_scales, w1, w2, gs, off
             num_t.append(bank)
         rows = out.rearrange("(p t) j -> p t j", t=PACK)
         all_logs = keep.tile([P, PACK, 2, S], F32, name="all_logs", tag="w2_raw1", align_bytes=64)
-        for t in range(PACK):
-            logs = all_logs[:, t]
-            nc.scalar.activation(logs[:, 0, :], num_t[t][:], ACT.Ln)
+        back = []
+
+        def log_numerator(t):
+            nc.scalar.activation(all_logs[:, t, 0, :], num_t[t][:], ACT.Ln)
             bank = psum.tile([P, S], F32, name="bank_l%d" % t, tag="bank%d" % t)
             for c in range(S // P):
                 cols = slice(c * P, (c + 1) * P)
-                nc.tensor.transpose(bank[:, cols], logs[:, 0, cols], ident[:])
+                nc.tensor.transpose(bank[:, cols], all_logs[:, t, 0, cols], ident[:])
+            back.append(bank)
+
+        log_numerator(0)
+        for t in range(PACK):
+            if t + 1 < PACK:
+                log_numerator(t + 1)
             res = keep.tile([P, S], F32, name="res%d" % t)
             parts = 2 if t == PACK - 1 else 1
             for h in range(parts):
                 cols = slice(h * S // parts, (h + 1) * S // parts)
-                nc.scalar.activation(logs[:, 1, cols], den[t][:, cols], ACT.Ln)
-                nc.vector.tensor_tensor(res[:, cols], bank[:, cols], logs[:, 1, cols], ALU.subtract)
+                nc.scalar.activation(all_logs[:, t, 1, cols], den[t][:, cols], ACT.Ln)
+                nc.vector.tensor_tensor(res[:, cols], back[t][:, cols], all_logs[:, t, 1, cols], ALU.subtract)
                 nc.sync.dma_start(rows[:, t, cols], res[:, cols])

from contextlib import ExitStack

import concourse.mybir as mybir
from concourse.masks import make_identity

K, T, S, H, W, C = 512, 2048, 512, 512, 256, 512
P = 128
PACK = 4
FLOPS = 3 * 2 * K * H * S

F32 = mybir.dt.float32
BF16 = mybir.dt.bfloat16
I32 = mybir.dt.int32
U32 = mybir.dt.uint32
U16 = mybir.dt.uint16
U8 = mybir.dt.uint8
FP8X4 = mybir.dt.float8_e4m3fn_x4
ACT = mybir.ActivationFunctionType
ALU = mybir.AluOpType
SCALAR_TILES = (2, 3)


def tile_picked_twcputbodds_none_p_kernel(tc, x_words, x_scales, w1, w2, gs, offs, two, n1, n2, cand, n3, n4, n5, out):
    nc = tc.nc
    with ExitStack() as ctx:
        keep = ctx.enter_context(tc.tile_pool(name="keep", bufs=1))
        psum = ctx.enter_context(tc.psum_pool(name="psum", bufs=1))

        def load_list(src, name):
            tile = keep.tile(list(src.shape), U16, name=name)
            nc.sync.dma_start(tile[:], src)
            return tile

        def load_weight_half(w, half, name):
            raw = keep.tile([P, PACK, H // 2], F32, name=name, tag=name, align_bytes=64)
            cols = slice(half * H // 2, (half + 1) * H // 2)
            nc.sync.dma_start(raw[:], w.rearrange("(p j) c -> p j c", j=PACK)[:, :, cols])
            return raw

        words = keep.tile([P, T], I32, name="words", align_bytes=64)
        scales = keep.tile([P, T], U8, name="scales", align_bytes=64)
        nc.gpsimd.memset(scales[:, : T // 4].bitcast(I32), 0)
        nc.vector.memset(scales[:, T // 4 :].bitcast(I32), 0)
        offs_t = load_list(offs, "offs_t")
        two_t = load_list(two, "two_t")
        cand_t = load_list(cand, "cand_t")
        for q in range(4):
            nc.sync.dma_start(scales[32 * q : 32 * q + 4, :].bitcast(I32), x_scales[0, 4 * q : 4 * q + 4, :].bitcast(I32))
        w1_whole = keep.tile([P, PACK, H], F32, name="w1_whole")
        nc.sync.dma_start(w1_whole[:], w1.rearrange("(p j) c -> p j c", j=PACK))
        w1_raw = [w1_whole[:, :, h * H // 2 : (h + 1) * H // 2] for h in range(2)]
        nc.sync.dma_start(words[:], x_words[0].rearrange("p n r -> p (n r)").bitcast(I32))
        w2_raw = [load_weight_half(w2, h, "w2_raw%d" % h) for h in range(2)]
        n1_t = load_list(n1, "n1_t")
        n2_t = load_list(n2, "n2_t")
        gs_t = keep.tile([P, PACK], F32, name="gs_t")
        nc.sync.dma_start(gs_t[:], gs.rearrange("(p t) o -> p (t o)", t=PACK))
        n3_t = load_list(n3, "n3_t")
        n4_t = load_list(n4, "n4_t")
        n5_t = load_list(n5, "n5_t")

        ex = [keep.tile([P, S if t == PACK - 1 else 2 * S], F32, name="ex%d" % t) for t in range(PACK)]
        last_ab = keep.tile([P, S], F32, name="last_ab", tag="last_ab", align_bytes=64)
        ab = [ex[t][:, S:] for t in range(PACK - 1)] + [last_ab[:]]
        half_s = {t: w2_raw[i][:].rearrange("p j c -> p (j c)") for i, t in enumerate(SCALAR_TILES)}
        ident = keep.tile([P, P], F32, name="ident")
        make_identity(nc, ident[:])

        def gather_words(lst, name, tag):
            got = keep.tile([P, S], U32, name=name, tag=tag, align_bytes=64)
            nc.vector.tensor_copy(got[:], words[:].bitcast(U32).indirect(lst[:]))
            return got

        def gather_scales(lst, name, tag):
            got = keep.tile([P, S], U8, name=name, tag=tag, align_bytes=64)
            nc.vector.tensor_copy(got[:], scales[:].indirect(lst[:]))
            return got

        def round_weight(raw, name, movers):
            grouped = keep.tile([P, PACK, P, PACK], BF16, name=name, tag=name, align_bytes=64)
            for h in range(2):
                movers[h](
                    grouped[:, :, h * P // 2 : (h + 1) * P // 2, :].rearrange("p t m j -> p m j t"),
                    raw[h].rearrange("p j (m t) -> p m j t", t=PACK),
                )
            return grouped

        def quantize(flat, name):
            codes = keep.tile([P, S], U32, name=name + "_codes", align_bytes=64)
            plane = keep.tile([P, S], U8, name=name + "_plane", align_bytes=64)
            nc.vector.quantize_mx(out=codes[:].bitcast(FP8X4), scales=plane[:], in_=flat)
            return codes, plane

        def product(bank, t, lhs, rhs, places=slice(0, S)):
            cols = slice(t * P, (t + 1) * P)
            nc.tensor.matmul_mx(bank[:, places], lhsT=lhs[0][:, cols].bitcast(FP8X4), lhsT_scale=lhs[1][:, cols],
                                rhs=rhs[0][:, places].bitcast(FP8X4), rhs_scale=rhs[1][:, places], start=True, stop=True)

        xq_s = gather_scales(offs_t, "xq_s", "xq_s")
        xt_s = gather_scales(two_t, "xt_s", "xt_s")
        xc_plain = gather_scales(cand_t, "xc_plain", "xc_plain")
        xc_s = keep.tile([P, C], U8, name="xc_s", align_bytes=64)
        nc.vector.tensor_copy(xc_s[:].rearrange("p (t m) -> p t m", t=PACK), xc_plain[:].rearrange("p (m t) -> p t m", t=PACK))
        w1_g = round_weight(w1_raw, "w1_g", (nc.scalar.copy, nc.scalar.copy))
        w1_q = quantize(w1_g[:].rearrange("p t m j -> p (t m j)"), "w1")
        xq = (gather_words(offs_t, "xq_w", "xq_w"), xq_s)
        xt = (gather_words(two_t, "xt_w", "w1_g"), xt_s)
        w2_g = round_weight([r[:] for r in w2_raw], "w2_g", (nc.scalar.copy, nc.scalar.copy))

        y = [keep.tile([P, S + 1 if t < 2 else S], F32, name="y%d" % t) for t in range(PACK)]
        for t in range(2):
            nc.gpsimd.tensor_copy(y[t][:, S:], gs_t[:, t + 2 : t + 3])
        d_gain = [gs_t[:, 0:1], gs_t[:, 1:2], y[0][:, S:], y[1][:, S:]]
        d = [keep.tile([P, S], F32, name="d%d" % t, tag="d%d" % t, align_bytes=64) for t in range(PACK)]
        a = [ab[t][:, :W] for t in range(PACK)]
        b = [ab[t][:, W:] for t in range(PACK)]
        for t in range(PACK):
            bank = psum.tile([P, S], F32, name="bank_y%d" % t, tag="bank%d" % t)
            product(bank, t, w1_q, xq)
            nc.scalar.activation(y[t][:, :S], bank[:], ACT.Copy, scale=gs_t[:, t : t + 1])
        nc.vector.tensor_scalar(a[0], y[0][:].indirect(n1_t[:]), -0.5, 0.0, ALU.mult, ALU.add)
        w2_q = quantize(w2_g[:].rearrange("p t m j -> p (t m j)"), "w2")
        for t in range(1, PACK):
            nc.vector.tensor_scalar(a[t], y[t][:].indirect(n1_t[:]), -0.5, 0.0, ALU.mult, ALU.add)
        for t in range(PACK):
            bank = psum.tile([P, S], F32, name="bank_d%d" % t, tag="bank%d" % (PACK + t))
            product(bank, t, w2_q, xt)
            nc.scalar.activation(d[t][:], bank[:], ACT.Copy, scale=d_gain[t])
        z_g = keep.tile([P, S, PACK], BF16, name="z_g", align_bytes=64)
        nc.vector.tensor_copy(b[0], d[0][:].indirect(n2_t[:]))
        for t in range(PACK):
            if t + 1 < PACK:
                nc.vector.tensor_copy(b[t + 1], d[t + 1][:].indirect(n2_t[:]))
            nc.vector.tensor_tensor(y[t][:].indirect(n1_t[:]), a[t], b[t], ALU.add)
            parts = 2 if t == PACK - 1 else 1
            for h in range(parts):
                cols = slice(h * S // parts, (h + 1) * S // parts)
                nc.scalar.copy(z_g[:, cols, t], y[t][:, cols])

        xc_w = keep.tile([P, C], U32, name="xc_w", tag="last_ab", align_bytes=64)
        nc.vector.tensor_copy(xc_w[:].rearrange("p (t m) -> p m t", t=PACK), words[:].bitcast(U32).indirect(cand_t[:]))
        z_codes = keep.tile([P, S], U32, name="z_codes", align_bytes=64)
        z_plane = keep.tile([P, S], U8, name="z_plane", align_bytes=64)
        for h in range(2):
            cols = slice(h * S // 2, (h + 1) * S // 2)
            nc.vector.quantize_mx(out=z_codes[:, cols].bitcast(FP8X4), scales=z_plane[:, cols], in_=z_g[:, cols, :].rearrange("p j t -> p (j t)"))
        z_q = (z_codes, z_plane)

        e4 = [keep.tile([P, S], F32, name="e4_%d" % t) for t in range(PACK)]
        e3 = [keep.tile([P, S], F32, name="e3_%d" % t) for t in range(PACK)]
        den = [keep.tile([P, S], F32, name="den%d" % t) for t in range(PACK)]
        banks = [psum.tile([P, S], F32, name="bank_s%d" % t, tag="bank%d" % t) for t in range(PACK)]
        for h in range(2):
            for t in (2, 0):
                product(banks[t], t, (xc_w, xc_s), z_q, slice(h * S // 2, (h + 1) * S // 2))
        for t in (1, 3):
            product(banks[t], t, (xc_w, xc_s), z_q)
        nc.vector.tensor_scalar(half_s[2][:, :S], banks[2][:], 0.03125, None, ALU.mult)
        for t in (0, 2, 1, 3):
            nc.scalar.activation(ex[t][:, :S], banks[t][:], ACT.Exp, scale=0.03125)
        nc.scalar.activation(half_s[3][:, :S], banks[3][:], ACT.Copy, scale=0.03125)
        for t in SCALAR_TILES:
            nc.scalar.activation(e4[t][:], half_s[t].indirect(n4_t[:]), ACT.Exp)
            nc.scalar.activation(e3[t][:], half_s[t].indirect(n3_t[:]), ACT.Exp)
        num_t = []
        for t in range(PACK):
            if t not in SCALAR_TILES:
                nc.vector.tensor_copy(e4[t][:], ex[t][:].indirect(n4_t[:]))
                nc.vector.tensor_copy(e3[t][:], ex[t][:].indirect(n3_t[:]))
            parts = 2 if t == PACK - 1 else 1
            for h in range(parts):
                cols = slice(h * S // parts, (h + 1) * S // parts)
                entries = slice(h * S // parts // 16, (h + 1) * S // parts // 16)
                nc.vector.tensor_tensor(den[t][:, cols], ex[t][:].indirect(n5_t[:, entries]), e4[t][:, cols], ALU.add)
            bank = psum.tile([P, S], F32, name="bank_n%d" % t, tag="bank%d" % (PACK + t))
            for c in range(S // P):
                cols = slice(c * P, (c + 1) * P)
                nc.tensor.matmul(bank[:, cols], ex[t][:, cols], ident[:], start=True, stop=False, is_transpose=True)
                nc.tensor.matmul(bank[:, cols], e3[t][:, cols], ident[:], start=False, stop=True, is_transpose=True)
            num_t.append(bank)
        rows = out.rearrange("(p t) j -> p t j", t=PACK)
        all_logs = keep.tile([P, PACK, 2, S], F32, name="all_logs", tag="w2_raw1", align_bytes=64)
        back = []

        def log_numerator(t):
            nc.scalar.activation(all_logs[:, t, 0, :], num_t[t][:], ACT.Ln)
            bank = psum.tile([P, S], F32, name="bank_l%d" % t, tag="bank%d" % t)
            for c in range(S // P):
                cols = slice(c * P, (c + 1) * P)
                nc.tensor.transpose(bank[:, cols], all_logs[:, t, 0, cols], ident[:])
            back.append(bank)

        log_numerator(0)
        for t in range(PACK):
            if t + 1 < PACK:
                log_numerator(t + 1)
            res = keep.tile([P, S], F32, name="res%d" % t)
            parts = 2 if t == PACK - 1 else 1
            for h in range(parts):
                cols = slice(h * S // parts, (h + 1) * S // parts)
                nc.scalar.activation(all_logs[:, t, 1, cols], den[t][:, cols], ACT.Ln)
                nc.vector.tensor_tensor(res[:, cols], back[t][:, cols], all_logs[:, t, 1, cols], ALU.subtract)
                nc.sync.dma_start(rows[:, t, cols], res[:, cols])
